import numpy as np
import ml_dtypes


def mxq(x, axis, fmt="e4m3"):
    dtype, down = {"e4m3": (ml_dtypes.float8_e4m3fn, 7), "e5m2": (ml_dtypes.float8_e5m2, 14)}[fmt]
    v = np.moveaxis(np.asarray(x, np.float32).astype(ml_dtypes.bfloat16).astype(np.float64), axis, -1)
    blocks = v.reshape(v.shape[:-1] + (-1, 32))
    amax = np.abs(blocks).max(-1, keepdims=True)
    byte = np.maximum(np.where(amax > 0, np.frexp(amax)[1] - 1 + 127, 0) - down, 1)
    scale = np.exp2(byte - 127.0)
    codes = (blocks / scale).astype(np.float32).astype(dtype).astype(np.float64)
    return np.moveaxis((codes * scale).reshape(v.shape), -1, axis)


WIDE = False


def mx_kscale(k, group=512):
    if not WIDE:
        return np.ones(k)
    levels = np.array([10, -10, 5, -5, 0])
    if group != 512:
        return np.exp2(np.random.permutation(np.resize(levels, k // group))).repeat(group)
    if k % 512:
        return np.exp2(np.random.permutation(np.resize(levels, k // 32))).repeat(32)
    a = np.empty((k // 512, 16))
    for p in range(k // 512):
        a[p, :8] = np.random.permutation(np.resize(levels, 8))
        for g in range(8):
            far = levels[np.abs(levels - a[p, g]) >= 10]
            a[p, g + 8] = far[np.random.randint(len(far))]
    return np.exp2(a.ravel()).repeat(32)


def f64(x):
    return np.asarray(x).astype(np.float64)


def silu(v):
    return v / (1.0 + np.exp(-v))


def sigmoid(v):
    return 1.0 / (1.0 + np.exp(-v))


G, D, M, N = 2, 256, 128, 512


def setup_inputs():
    n = np.random.standard_normal
    s_d = mx_kscale(D, 0)
    return {
        "x": (n((G, D, N)) * s_d[:, None]).astype(np.float32),
        "w1": (n((G, D, M)) / np.sqrt(D) / s_d[:, None]).astype(np.float32),
        "w2": (n((G, D, M)) / np.sqrt(D) / s_d[:, None]).astype(np.float32),
        "w3": (n((G, D, M)) / np.sqrt(D) / s_d[:, None]).astype(np.float32),
        "b3": (0.5 * n((G, M, 1))).astype(np.float32),
        "dx": (n((G, D, N)) * s_d[:, None]).astype(np.float32),
        "og": (np.random.uniform(0.5, 2.0, (G, M, 1))).astype(np.float32),
        "base": (0.3 * n((G, M, N))).astype(np.float32),
    }


def reference(x, w1, w2, w3, b3, dx, og, base):
    w1q = mxq(f64(w1), 1, "e4m3")
    xq = mxq(f64(x), 1, "e4m3")
    z1 = w1q.transpose(0, 2, 1) @ xq
    dxq = mxq(f64(dx), 1, "e4m3")
    tz1 = w1q.transpose(0, 2, 1) @ dxq
    w2q = mxq(f64(w2), 1, "e4m3")
    z2 = w2q.transpose(0, 2, 1) @ xq
    tz2 = w2q.transpose(0, 2, 1) @ dxq
    w3q = mxq(f64(w3), 1, "e4m3")
    z3 = w3q.transpose(0, 2, 1) @ xq
    tz3 = w3q.transpose(0, 2, 1) @ dxq
    e1 = np.tanh(z1)
    e2 = silu(z2)
    gt = sigmoid(z3 + f64(b3))
    xe1 = tz1 * (1.0 - np.square(e1))
    xe2 = tz2 * sigmoid(z2) * (1.0 + z2 * (1.0 - sigmoid(z2)))
    xgt = tz3 * gt * (1.0 - gt)
    xh = xe2 + xgt * (e1 - e2) + (xe1 - xe2) * gt
    y = xh * f64(og) + f64(base)
    return y

@@ -1,0 +1,269 @@
+from contextlib import ExitStack
+
+import concourse.mybir as mybir
+
+G, D, M, N = 2, 256, 128, 512
+FLOPS = 6 * 2 * G * D * M * N
+
+F32 = mybir.dt.float32
+BF16 = mybir.dt.bfloat16
+U32 = mybir.dt.uint32
+U8 = mybir.dt.uint8
+FP8X4 = mybir.dt.float8_e4m3fn_x4
+ACT = mybir.ActivationFunctionType
+ALU = mybir.AluOpType
+
+P = 128
+PACK = 4
+ROWS = D // PACK
+W = 128
+CHUNKS = N // W
+BANK = 512
+
+
+def tile_rows_tnmixture_kernel(tc, x, w1, w2, w3, b3, dx, og, base, out):
+    nc = tc.nc
+    with ExitStack() as ctx:
+        sb = ctx.enter_context(tc.tile_pool(name="sb", bufs=1))
+        ps = ctx.enter_context(tc.psum_pool(name="ps", bufs=1))
+        ctx.enter_context(tc.manual_schedule())
+
+        def load(name, src, c0, c1):
+            raw = sb.tile([P, PACK, c1 - c0], F32, name=name + "_raw")
+            nc.sync.dma_start(out=raw[:], in_=src.rearrange("g (p j) n -> (g p) j n", j=PACK)[:, :, c0:c1])
+            return raw
+
+        def load_col(name, src):
+            col = sb.tile([P, G], F32, name=name)
+            with nc.allow_non_contiguous_dma(reason="one value a partition"):
+                nc.sync.dma_start(out=col[:], in_=src.rearrange("g m o -> m (g o)"))
+            return col
+
+        raw = {}
+        raw["x0"] = load("x0", x, 0, W)[:]
+        raw["w0"] = load("w0", w1, 0, M)[:]
+        raw["d0"] = load("d0", dx, 0, W)[:]
+        raw["w1"] = load("w1", w2, 0, M)[:]
+        b3_col = load_col("b3_col", b3)
+        raw["w2"] = load("w2", w3, 0, M)[:]
+        raw["x1"] = load("x1", x, W, 2 * W)[:]
+        raw["d1"] = load("d1", dx, W, 2 * W)[:]
+        og_col = load_col("og_col", og)
+        base_lo = sb.tile([P, G, 2 * W], F32, name="base_lo")
+        nc.sync.dma_start(out=base_lo[:], in_=base.rearrange("g m n -> m g n")[:, :, 0 : 2 * W])
+        x23 = load("x23", x, 2 * W, N)
+        d23 = load("d23", dx, 2 * W, N)
+        raw["x2"] = x23[:, :, 0:W]
+        raw["x3"] = x23[:, :, W : 2 * W]
+        raw["d2"] = d23[:, :, 0:W]
+        raw["d3"] = d23[:, :, W : 2 * W]
+        base_hi = sb.tile([P, G, 2 * W], F32, name="base_hi")
+        nc.sync.dma_start(out=base_hi[:], in_=base.rearrange("g m n -> m g n")[:, :, 2 * W : N])
+        base_sb = [(base_lo, base_hi)[c // 2][:, :, (c % 2) * W : (c % 2 + 1) * W] for c in range(CHUNKS)]
+
+        grouped, codes, scales = {}, {}, {}
+
+        def interleave(name, on_scalar=False):
+            grouped[name] = sb.tile([P, W, PACK], BF16, name=name + "_bf", align_bytes=64)
+            dst = grouped[name][:].rearrange("p (c i) j -> p c j i", i=4)
+            src = raw[name].rearrange("p j (c i) -> p c j i", i=4)
+            if on_scalar:
+                nc.scalar.copy(out=dst, in_=src)
+            else:
+                nc.vector.tensor_copy(out=dst, in_=src)
+
+        def quantize(name):
+            codes[name] = sb.tile([P, W], U32, name=name + "_codes", align_bytes=64)
+            scales[name] = sb.tile([P, W], U8, name=name + "_scales", align_bytes=64)
+            nc.vector.quantize_mx(
+                out=codes[name][:].bitcast(FP8X4),
+                scales=scales[name][:],
+                in_=grouped[name][:].rearrange("p n j -> p (n j)"),
+            )
+
+        z_banks = [[ps.tile([P, BANK], F32, name="z%d%d" % (g, s)) for s in range(2)] for g in range(G)]
+        t_banks = [[ps.tile([P, BANK], F32, name="t%d%d" % (g, s)) for s in range(2)] for g in range(G)]
+
+        def place(banks, c, g, k):
+            s = 0 if (c == 0 and k == 1) else (c + 1) % 2
+            return banks[g][s][:, k * W : (k + 1) * W]
+
+        def product(kind, c, g, k):
+            rows = slice(g * ROWS, (g + 1) * ROWS)
+            wn, mn = "w%d" % k, "%s%d" % (kind, c)
+            nc.tensor.matmul_mx(
+                out=place(z_banks if kind == "x" else t_banks, c, g, k),
+                lhsT=codes[wn][rows, :].bitcast(FP8X4),
+                lhsT_scale=scales[wn][rows, :],
+                rhs=codes[mn][rows, :].bitcast(FP8X4),
+                rhs_scale=scales[mn][rows, :],
+                start=True,
+                stop=True,
+            )
+
+        def products(kind, c, ks=(0, 1, 2)):
+            for g in range(G):
+                for k in ks:
+                    product(kind, c, g, k)
+
+        def per_chunk(name, inner=1):
+            return [sb.tile([P, G, inner, W], F32, name="%s%d" % (name, c)) for c in range(CHUNKS)]
+
+        fac = per_chunk("fac", 3)
+        prod = per_chunk("prod", 3)
+        e1, e2, mneg = per_chunk("e1"), per_chunk("e2"), per_chunk("mneg")
+        bb, cc, ww, vv, uu = per_chunk("bb"), per_chunk("cc"), per_chunk("ww"), per_chunk("vv"), per_chunk("uu")
+        gr, xh, yy = per_chunk("gr"), per_chunk("xh"), per_chunk("yy")
+        half_b = sb.tile([P, G], F32, name="half_b")
+        og_q = sb.tile([P, G], F32, name="og_q")
+        warm = sb.tile([P, 2], F32, name="warm")
+
+        def a_e1(c, g):
+            nc.scalar.activation(out=e1[c][:, g, 0, :], in_=place(z_banks, c, g, 0), func=ACT.Tanh)
+
+        def a_sq(c, g):
+            nc.scalar.activation(out=fac[c][:, g, 0, :], in_=e1[c][:, g, 0, :], func=ACT.Square)
+
+        def a_t2(c, g):
+            nc.scalar.activation(out=fac[c][:, g, 1, :], in_=place(z_banks, c, g, 1), func=ACT.Tanh, scale=-0.5)
+
+        def a_t3(c, g):
+            nc.scalar.activation(
+                out=fac[c][:, g, 2, :], in_=place(z_banks, c, g, 2), func=ACT.Tanh, scale=0.5, bias=half_b[:, g : g + 1]
+            )
+
+        def a_m(c, g):
+            nc.scalar.activation(out=mneg[c][:, g, 0, :], in_=place(z_banks, c, g, 1), func=ACT.Silu, scale=-1.0)
+
+        def a_e2(c, g):
+            nc.scalar.activation(out=e2[c][:, g, 0, :], in_=place(z_banks, c, g, 1), func=ACT.Silu)
+
+        def acts(c):
+            for g in range(G):
+                a_e1(c, g)
+                a_t2(c, g)
+                a_t3(c, g)
+                a_sq(c, g)
+            for f in (a_e2, a_m):
+                for g in range(G):
+                    f(c, g)
+
+        def stt(o, a, s, b, op0, op1):
+            nc.vector.scalar_tensor_tensor(out=o, in0=a, scalar=s, in1=b, op0=op0, op1=op1)
+
+        def v_p1(c, g, k):
+            stt(prod[c][:, g, k, :], fac[c][:, g, k, :], 1.0, place(t_banks, c, g, k), ALU.subtract, ALU.mult)
+
+        def v_p(c, g):
+            stt(
+                prod[c][:, g].rearrange("p k n -> p (k n)"),
+                fac[c][:, g].rearrange("p k n -> p (k n)"),
+                1.0,
+                t_banks[g][(c + 1) % 2][:, 0 : 3 * W],
+                ALU.subtract,
+                ALU.mult,
+            )
+
+        def v_b(c):
+            stt(bb[c][:, :, 0, :], mneg[c][:, :, 0, :], 1.0, prod[c][:, :, 1, :], ALU.subtract, ALU.mult)
+
+        def v_c(c):
+            nc.vector.tensor_tensor(out=cc[c][:, :, 0, :], in0=e1[c][:, :, 0, :], in1=e2[c][:, :, 0, :], op=ALU.subtract)
+
+        def v_w(c):
+            stt(ww[c][:, :, 0, :], cc[c][:, :, 0, :], -0.25, prod[c][:, :, 2, :], ALU.mult, ALU.mult)
+
+        def v_v(c, gs=slice(0, G)):
+            stt(vv[c][:, gs, 0, :], prod[c][:, gs, 0, :], -0.5, ww[c][:, gs, 0, :], ALU.mult, ALU.add)
+
+        def v_h(c):
+            stt(uu[c][:, :, 0, :], fac[c][:, :, 2, :], 1.0, bb[c][:, :, 0, :], ALU.subtract, ALU.mult)
+
+        def v_g(c):
+            stt(gr[c][:, :, 0, :], fac[c][:, :, 2, :], 1.0, vv[c][:, :, 0, :], ALU.add, ALU.mult)
+
+        def v_x(c):
+            for g in range(G):
+                stt(xh[c][:, g, 0, :], uu[c][:, g, 0, :], og_q[:, g : g + 1], base_sb[c][:, g, :], ALU.mult, ALU.add)
+
+        def v_y(c):
+            for g in range(G):
+                stt(yy[c][:, g, 0, :], gr[c][:, g, 0, :], og_col[:, g : g + 1], xh[c][:, g, 0, :], ALU.mult, ALU.add)
+            nc.sync.dma_start(out=out.rearrange("g m n -> m g n")[:, :, c * W : (c + 1) * W], in_=yy[c][:, :, 0, :])
+
+        nc.gpsimd.memset(warm[:, 0:1], 0.0)
+        nc.scalar.activation(out=warm[:, 1:2], in_=warm[:, 0:1], func=ACT.Silu)
+        interleave("x0")
+        quantize("x0")
+        interleave("w0")
+        interleave("d0", on_scalar=True)
+        quantize("w0")
+        products("x", 0, (0,))
+        for f in (a_e1, a_sq):
+            for g in range(G):
+                f(0, g)
+        interleave("w1")
+        quantize("d0")
+        products("d", 0, (0,))
+        quantize("w1")
+        products("x", 0, (1,))
+        products("d", 0, (1,))
+        for f in (a_t2, a_m):
+            for g in range(G):
+                f(0, g)
+        nc.scalar.activation(out=half_b[:], in_=b3_col[:], func=ACT.Copy, scale=0.5)
+        interleave("w2")
+        v_p1(0, 0, 0)
+        v_p1(0, 1, 0)
+        quantize("w2")
+        for g in range(G):
+            a_e2(0, g)
+        v_p1(0, 0, 1)
+        v_p1(0, 1, 1)
+        products("x", 0, (2,))
+        products("d", 0, (2,))
+        for g in range(G):
+            a_t3(0, g)
+        interleave("x1")
+        v_b(0)
+        quantize("x1")
+        products("x", 1)
+        v_c(0)
+        v_p1(0, 0, 2)
+        v_p1(0, 1, 2)
+        interleave("d1", on_scalar=True)
+        nc.scalar.activation(out=og_q[:], in_=og_col[:], func=ACT.Copy, scale=-0.25)
+        acts(1)
+        v_h(0)
+        v_w(0)
+        quantize("d1")
+        products("d", 1)
+        v_v(0)
+        v_x(0)
+        v_g(0)
+
+        interleave("x2", on_scalar=True)
+        interleave("d2", on_scalar=True)
+        interleave("x3", on_scalar=True)
+        for c in range(1, CHUNKS):
+            last = c == CHUNKS - 1
+            v_p(c, 0)
+            v_y(c - 1)
+            v_p(c, 1)
+            v_c(c)
+            if not last:
+                quantize("x%d" % (c + 1))
+                products("x", c + 1)
+                acts(c + 1)
+            if c == 1:
+                interleave("d3", on_scalar=True)
+            v_b(c)
+            v_w(c)
+            if not last:
+                quantize("d%d" % (c + 1))
+                products("d", c + 1)
+            v_h(c)
+            v_v(c)
+            v_x(c)
+            v_g(c)
+        v_y(CHUNKS - 1)

@@ -48,11 +48,11 @@ def tile_rows_tnmixture_kernel(tc, x, w1, w2, w3, b3, dx, og, base, out):
         raw["w2"] = load("w2", w3, 0, M)[:]
         raw["x1"] = load("x1", x, W, 2 * W)[:]
         raw["d1"] = load("d1", dx, W, 2 * W)[:]
+        x23 = load("x23", x, 2 * W, N)
+        d23 = load("d23", dx, 2 * W, N)
         og_col = load_col("og_col", og)
         base_lo = sb.tile([P, G, 2 * W], F32, name="base_lo")
         nc.sync.dma_start(out=base_lo[:], in_=base.rearrange("g m n -> m g n")[:, :, 0 : 2 * W])
-        x23 = load("x23", x, 2 * W, N)
-        d23 = load("d23", dx, 2 * W, N)
         raw["x2"] = x23[:, :, 0:W]
         raw["x3"] = x23[:, :, W : 2 * W]
         raw["d2"] = d23[:, :, 0:W]
@@ -144,9 +144,17 @@ def tile_rows_tnmixture_kernel(tc, x, w1, w2, w3, b3, dx, og, base, out):
                 a_t2(c, g)
                 a_t3(c, g)
                 a_sq(c, g)
-            for f in (a_e2, a_m):
-                for g in range(G):
-                    f(c, g)
+            for g in range(G):
+                a_e2(c, g)
+            if c == 1:
+                interleave("x2", on_scalar=True)
+            for g in range(G):
+                a_m(c, g)
+            if c + 1 < CHUNKS:
+                interleave("d%d" % (c + 1), on_scalar=True)
+            if c == 1:
+                nc.scalar.activation(out=og_q[:], in_=og_col[:], func=ACT.Copy, scale=0.25)
+                interleave("x3", on_scalar=True)
 
         def stt(o, a, s, b, op0, op1):
             nc.vector.scalar_tensor_tensor(out=o, in0=a, scalar=s, in1=b, op0=op0, op1=op1)
@@ -171,24 +179,23 @@ def tile_rows_tnmixture_kernel(tc, x, w1, w2, w3, b3, dx, og, base, out):
             nc.vector.tensor_tensor(out=cc[c][:, :, 0, :], in0=e1[c][:, :, 0, :], in1=e2[c][:, :, 0, :], op=ALU.subtract)
 
         def v_w(c):
-            stt(ww[c][:, :, 0, :], cc[c][:, :, 0, :], -0.25, prod[c][:, :, 2, :], ALU.mult, ALU.mult)
+            stt(ww[c][:, :, 0, :], cc[c][:, :, 0, :], -1.0, prod[c][:, :, 2, :], ALU.mult, ALU.mult)
 
         def v_v(c, gs=slice(0, G)):
-            stt(vv[c][:, gs, 0, :], prod[c][:, gs, 0, :], -0.5, ww[c][:, gs, 0, :], ALU.mult, ALU.add)
+            stt(vv[c][:, gs, 0, :], prod[c][:, gs, 0, :], -2.0, ww[c][:, gs, 0, :], ALU.mult, ALU.add)
 
         def v_h(c):
             stt(uu[c][:, :, 0, :], fac[c][:, :, 2, :], 1.0, bb[c][:, :, 0, :], ALU.subtract, ALU.mult)
 
-        def v_g(c):
-            stt(gr[c][:, :, 0, :], fac[c][:, :, 2, :], 1.0, vv[c][:, :, 0, :], ALU.add, ALU.mult)
+        def v_g(c, gs=slice(0, G)):
+            stt(gr[c][:, gs, 0, :], fac[c][:, gs, 2, :], 1.0, vv[c][:, gs, 0, :], ALU.add, ALU.mult)
 
-        def v_x(c):
-            for g in range(G):
-                stt(xh[c][:, g, 0, :], uu[c][:, g, 0, :], og_q[:, g : g + 1], base_sb[c][:, g, :], ALU.mult, ALU.add)
+        def mix(c):
+            nc.gpsimd.tensor_tensor(out=xh[c][:, :, 0, :], in0=gr[c][:, :, 0, :], in1=uu[c][:, :, 0, :], op=ALU.subtract)
 
         def v_y(c):
             for g in range(G):
-                stt(yy[c][:, g, 0, :], gr[c][:, g, 0, :], og_col[:, g : g + 1], xh[c][:, g, 0, :], ALU.mult, ALU.add)
+                stt(yy[c][:, g, 0, :], xh[c][:, g, 0, :], og_q[:, g : g + 1], base_sb[c][:, g, :], ALU.mult, ALU.add)
             nc.sync.dma_start(out=out.rearrange("g m n -> m g n")[:, :, c * W : (c + 1) * W], in_=yy[c][:, :, 0, :])
 
         nc.gpsimd.memset(warm[:, 0:1], 0.0)
@@ -208,7 +215,7 @@ def tile_rows_tnmixture_kernel(tc, x, w1, w2, w3, b3, dx, og, base, out):
         quantize("w1")
         products("x", 0, (1,))
         products("d", 0, (1,))
-        for f in (a_t2, a_m):
+        for f in (a_t2, a_e2):
             for g in range(G):
                 f(0, g)
         nc.scalar.activation(out=half_b[:], in_=b3_col[:], func=ACT.Copy, scale=0.5)
@@ -217,53 +224,57 @@ def tile_rows_tnmixture_kernel(tc, x, w1, w2, w3, b3, dx, og, base, out):
         v_p1(0, 1, 0)
         quantize("w2")
         for g in range(G):
-            a_e2(0, g)
+            a_m(0, g)
+        interleave("x1")
         v_p1(0, 0, 1)
         v_p1(0, 1, 1)
         products("x", 0, (2,))
         products("d", 0, (2,))
         for g in range(G):
             a_t3(0, g)
-        interleave("x1")
-        v_b(0)
         quantize("x1")
         products("x", 1)
         v_c(0)
         v_p1(0, 0, 2)
         v_p1(0, 1, 2)
         interleave("d1", on_scalar=True)
-        nc.scalar.activation(out=og_q[:], in_=og_col[:], func=ACT.Copy, scale=-0.25)
         acts(1)
-        v_h(0)
+        v_b(0)
         v_w(0)
         quantize("d1")
         products("d", 1)
         v_v(0)
-        v_x(0)
+        v_h(0)
         v_g(0)
 
-        interleave("x2", on_scalar=True)
-        interleave("d2", on_scalar=True)
-        interleave("x3", on_scalar=True)
+        def next_x(c):
+            quantize("x%d" % c)
+            products("x", c)
+            acts(c)
+
         for c in range(1, CHUNKS):
-            last = c == CHUNKS - 1
+            mix(c - 1)
+            if c == 2:
+                next_x(3)
             v_p(c, 0)
-            v_y(c - 1)
             v_p(c, 1)
             v_c(c)
-            if not last:
-                quantize("x%d" % (c + 1))
-                products("x", c + 1)
-                acts(c + 1)
             if c == 1:
-                interleave("d3", on_scalar=True)
+                next_x(2)
             v_b(c)
             v_w(c)
-            if not last:
+            if c + 1 < CHUNKS:
                 quantize("d%d" % (c + 1))
                 products("d", c + 1)
-            v_h(c)
+            v_y(c - 1)
             v_v(c)
-            v_x(c)
-            v_g(c)
-        v_y(CHUNKS - 1)
+            v_h(c)
+            if c + 1 < CHUNKS:
+                v_g(c)
+        c = CHUNKS - 1
+        v_g(c)
+        for g in range(G):
+            stt(xh[c][:, g, 0, :], uu[c][:, g, 0, :], og_q[:, g : g + 1], base_sb[c][:, g, :], ALU.mult, ALU.subtract)
+        for g in range(G):
+            stt(yy[c][:, g, 0, :], gr[c][:, g, 0, :], og_q[:, g : g + 1], xh[c][:, g, 0, :], ALU.mult, ALU.subtract)
+        nc.sync.dma_start(out=out.rearrange("g m n -> m g n")[:, :, c * W : (c + 1) * W], in_=yy[c][:, :, 0, :])

@@ -40,13 +40,13 @@ def tile_rows_tnmixture_kernel(tc, x, w1, w2, w3, b3, dx, og, base, out):
             return col
 
         raw = {}
-        raw["x0"] = load("x0", x, 0, W)[:]
         raw["w0"] = load("w0", w1, 0, M)[:]
+        raw["x0"] = load("x0", x, 0, W)[:]
         raw["d0"] = load("d0", dx, 0, W)[:]
         raw["w1"] = load("w1", w2, 0, M)[:]
-        b3_col = load_col("b3_col", b3)
         raw["w2"] = load("w2", w3, 0, M)[:]
         raw["x1"] = load("x1", x, W, 2 * W)[:]
+        b3_col = load_col("b3_col", b3)
         raw["d1"] = load("d1", dx, W, 2 * W)[:]
         x23 = load("x23", x, 2 * W, N)
         d23 = load("d23", dx, 2 * W, N)
@@ -200,11 +200,11 @@ def tile_rows_tnmixture_kernel(tc, x, w1, w2, w3, b3, dx, og, base, out):
 
         nc.gpsimd.memset(warm[:, 0:1], 0.0)
         nc.scalar.activation(out=warm[:, 1:2], in_=warm[:, 0:1], func=ACT.Silu)
-        interleave("x0")
-        quantize("x0")
         interleave("w0")
-        interleave("d0", on_scalar=True)
         quantize("w0")
+        interleave("x0")
+        interleave("d0", on_scalar=True)
+        quantize("x0")
         products("x", 0, (0,))
         for f in (a_e1, a_sq):
             for g in range(G):
@@ -277,4 +277,4 @@ def tile_rows_tnmixture_kernel(tc, x, w1, w2, w3, b3, dx, og, base, out):
             stt(xh[c][:, g, 0, :], uu[c][:, g, 0, :], og_q[:, g : g + 1], base_sb[c][:, g, :], ALU.mult, ALU.subtract)
         for g in range(G):
             stt(yy[c][:, g, 0, :], gr[c][:, g, 0, :], og_q[:, g : g + 1], xh[c][:, g, 0, :], ALU.mult, ALU.subtract)
-        nc.sync.dma_start(out=out.rearrange("g m n -> m g n")[:, :, c * W : (c + 1) * W], in_=yy[c][:, :, 0, :])
+            nc.sync.dma_start(out=out[g, :, c * W : (c + 1) * W], in_=yy[c][:, g, 0, :])

from contextlib import ExitStack

import concourse.mybir as mybir

G, D, M, N = 2, 256, 128, 512
FLOPS = 6 * 2 * G * D * M * N

F32 = mybir.dt.float32
BF16 = mybir.dt.bfloat16
U32 = mybir.dt.uint32
U8 = mybir.dt.uint8
FP8X4 = mybir.dt.float8_e4m3fn_x4
ACT = mybir.ActivationFunctionType
ALU = mybir.AluOpType

P = 128
PACK = 4
ROWS = D // PACK
W = 128
CHUNKS = N // W
BANK = 512


def tile_rows_tnmixture_kernel(tc, x, w1, w2, w3, b3, dx, og, base, out):
    nc = tc.nc
    with ExitStack() as ctx:
        sb = ctx.enter_context(tc.tile_pool(name="sb", bufs=1))
        ps = ctx.enter_context(tc.psum_pool(name="ps", bufs=1))
        ctx.enter_context(tc.manual_schedule())

        def load(name, src, c0, c1):
            raw = sb.tile([P, PACK, c1 - c0], F32, name=name + "_raw")
            nc.sync.dma_start(out=raw[:], in_=src.rearrange("g (p j) n -> (g p) j n", j=PACK)[:, :, c0:c1])
            return raw

        def load_col(name, src):
            col = sb.tile([P, G], F32, name=name)
            with nc.allow_non_contiguous_dma(reason="one value a partition"):
                nc.sync.dma_start(out=col[:], in_=src.rearrange("g m o -> m (g o)"))
            return col

        raw = {}
        raw["w0"] = load("w0", w1, 0, M)[:]
        raw["x0"] = load("x0", x, 0, W)[:]
        raw["d0"] = load("d0", dx, 0, W)[:]
        raw["w1"] = load("w1", w2, 0, M)[:]
        raw["w2"] = load("w2", w3, 0, M)[:]
        raw["x1"] = load("x1", x, W, 2 * W)[:]
        b3_col = load_col("b3_col", b3)
        raw["d1"] = load("d1", dx, W, 2 * W)[:]
        x23 = load("x23", x, 2 * W, N)
        d23 = load("d23", dx, 2 * W, N)
        og_col = load_col("og_col", og)
        base_lo = sb.tile([P, G, 2 * W], F32, name="base_lo")
        nc.sync.dma_start(out=base_lo[:], in_=base.rearrange("g m n -> m g n")[:, :, 0 : 2 * W])
        raw["x2"] = x23[:, :, 0:W]
        raw["x3"] = x23[:, :, W : 2 * W]
        raw["d2"] = d23[:, :, 0:W]
        raw["d3"] = d23[:, :, W : 2 * W]
        base_hi = sb.tile([P, G, 2 * W], F32, name="base_hi")
        nc.sync.dma_start(out=base_hi[:], in_=base.rearrange("g m n -> m g n")[:, :, 2 * W : N])
        base_sb = [(base_lo, base_hi)[c // 2][:, :, (c % 2) * W : (c % 2 + 1) * W] for c in range(CHUNKS)]

        grouped, codes, scales = {}, {}, {}

        def interleave(name, on_scalar=False):
            grouped[name] = sb.tile([P, W, PACK], BF16, name=name + "_bf", align_bytes=64)
            dst = grouped[name][:].rearrange("p (c i) j -> p c j i", i=4)
            src = raw[name].rearrange("p j (c i) -> p c j i", i=4)
            if on_scalar:
                nc.scalar.copy(out=dst, in_=src)
            else:
                nc.vector.tensor_copy(out=dst, in_=src)

        def quantize(name):
            codes[name] = sb.tile([P, W], U32, name=name + "_codes", align_bytes=64)
            scales[name] = sb.tile([P, W], U8, name=name + "_scales", align_bytes=64)
            nc.vector.quantize_mx(
                out=codes[name][:].bitcast(FP8X4),
                scales=scales[name][:],
                in_=grouped[name][:].rearrange("p n j -> p (n j)"),
            )

        z_banks = [[ps.tile([P, BANK], F32, name="z%d%d" % (g, s)) for s in range(2)] for g in range(G)]
        t_banks = [[ps.tile([P, BANK], F32, name="t%d%d" % (g, s)) for s in range(2)] for g in range(G)]

        def place(banks, c, g, k):
            s = 0 if (c == 0 and k == 1) else (c + 1) % 2
            return banks[g][s][:, k * W : (k + 1) * W]

        def product(kind, c, g, k):
            rows = slice(g * ROWS, (g + 1) * ROWS)
            wn, mn = "w%d" % k, "%s%d" % (kind, c)
            nc.tensor.matmul_mx(
                out=place(z_banks if kind == "x" else t_banks, c, g, k),
                lhsT=codes[wn][rows, :].bitcast(FP8X4),
                lhsT_scale=scales[wn][rows, :],
                rhs=codes[mn][rows, :].bitcast(FP8X4),
                rhs_scale=scales[mn][rows, :],
                start=True,
                stop=True,
            )

        def products(kind, c, ks=(0, 1, 2)):
            for g in range(G):
                for k in ks:
                    product(kind, c, g, k)

        def per_chunk(name, inner=1):
            return [sb.tile([P, G, inner, W], F32, name="%s%d" % (name, c)) for c in range(CHUNKS)]

        fac = per_chunk("fac", 3)
        prod = per_chunk("prod", 3)
        e1, e2, mneg = per_chunk("e1"), per_chunk("e2"), per_chunk("mneg")
        bb, cc, ww, vv, uu = per_chunk("bb"), per_chunk("cc"), per_chunk("ww"), per_chunk("vv"), per_chunk("uu")
        gr, xh, yy = per_chunk("gr"), per_chunk("xh"), per_chunk("yy")
        half_b = sb.tile([P, G], F32, name="half_b")
        og_q = sb.tile([P, G], F32, name="og_q")
        warm = sb.tile([P, 2], F32, name="warm")

        def a_e1(c, g):
            nc.scalar.activation(out=e1[c][:, g, 0, :], in_=place(z_banks, c, g, 0), func=ACT.Tanh)

        def a_sq(c, g):
            nc.scalar.activation(out=fac[c][:, g, 0, :], in_=e1[c][:, g, 0, :], func=ACT.Square)

        def a_t2(c, g):
            nc.scalar.activation(out=fac[c][:, g, 1, :], in_=place(z_banks, c, g, 1), func=ACT.Tanh, scale=-0.5)

        def a_t3(c, g):
            nc.scalar.activation(
                out=fac[c][:, g, 2, :], in_=place(z_banks, c, g, 2), func=ACT.Tanh, scale=0.5, bias=half_b[:, g : g + 1]
            )

        def a_m(c, g):
            nc.scalar.activation(out=mneg[c][:, g, 0, :], in_=place(z_banks, c, g, 1), func=ACT.Silu, scale=-1.0)

        def a_e2(c, g):
            nc.scalar.activation(out=e2[c][:, g, 0, :], in_=place(z_banks, c, g, 1), func=ACT.Silu)

        def acts(c):
            for g in range(G):
                a_e1(c, g)
                a_t2(c, g)
                a_t3(c, g)
                a_sq(c, g)
            for g in range(G):
                a_e2(c, g)
            if c == 1:
                interleave("x2", on_scalar=True)
            for g in range(G):
                a_m(c, g)
            if c + 1 < CHUNKS:
                interleave("d%d" % (c + 1), on_scalar=True)
            if c == 1:
                nc.scalar.activation(out=og_q[:], in_=og_col[:], func=ACT.Copy, scale=0.25)
                interleave("x3", on_scalar=True)

        def stt(o, a, s, b, op0, op1):
            nc.vector.scalar_tensor_tensor(out=o, in0=a, scalar=s, in1=b, op0=op0, op1=op1)

        def v_p1(c, g, k):
            stt(prod[c][:, g, k, :], fac[c][:, g, k, :], 1.0, place(t_banks, c, g, k), ALU.subtract, ALU.mult)

        def v_p(c, g):
            stt(
                prod[c][:, g].rearrange("p k n -> p (k n)"),
                fac[c][:, g].rearrange("p k n -> p (k n)"),
                1.0,
                t_banks[g][(c + 1) % 2][:, 0 : 3 * W],
                ALU.subtract,
                ALU.mult,
            )

        def v_b(c):
            stt(bb[c][:, :, 0, :], mneg[c][:, :, 0, :], 1.0, prod[c][:, :, 1, :], ALU.subtract, ALU.mult)

        def v_c(c):
            nc.vector.tensor_tensor(out=cc[c][:, :, 0, :], in0=e1[c][:, :, 0, :], in1=e2[c][:, :, 0, :], op=ALU.subtract)

        def v_w(c):
            stt(ww[c][:, :, 0, :], cc[c][:, :, 0, :], -1.0, prod[c][:, :, 2, :], ALU.mult, ALU.mult)

        def v_v(c, gs=slice(0, G)):
            stt(vv[c][:, gs, 0, :], prod[c][:, gs, 0, :], -2.0, ww[c][:, gs, 0, :], ALU.mult, ALU.add)

        def v_h(c):
            stt(uu[c][:, :, 0, :], fac[c][:, :, 2, :], 1.0, bb[c][:, :, 0, :], ALU.subtract, ALU.mult)

        def v_g(c, gs=slice(0, G)):
            stt(gr[c][:, gs, 0, :], fac[c][:, gs, 2, :], 1.0, vv[c][:, gs, 0, :], ALU.add, ALU.mult)

        def mix(c):
            nc.gpsimd.tensor_tensor(out=xh[c][:, :, 0, :], in0=gr[c][:, :, 0, :], in1=uu[c][:, :, 0, :], op=ALU.subtract)

        def v_y(c):
            for g in range(G):
                stt(yy[c][:, g, 0, :], xh[c][:, g, 0, :], og_q[:, g : g + 1], base_sb[c][:, g, :], ALU.mult, ALU.add)
            nc.sync.dma_start(out=out.rearrange("g m n -> m g n")[:, :, c * W : (c + 1) * W], in_=yy[c][:, :, 0, :])

        nc.gpsimd.memset(warm[:, 0:1], 0.0)
        nc.scalar.activation(out=warm[:, 1:2], in_=warm[:, 0:1], func=ACT.Silu)
        interleave("w0")
        quantize("w0")
        interleave("x0")
        interleave("d0", on_scalar=True)
        quantize("x0")
        products("x", 0, (0,))
        for f in (a_e1, a_sq):
            for g in range(G):
                f(0, g)
        interleave("w1")
        quantize("d0")
        products("d", 0, (0,))
        quantize("w1")
        products("x", 0, (1,))
        products("d", 0, (1,))
        for f in (a_t2, a_e2):
            for g in range(G):
                f(0, g)
        nc.scalar.activation(out=half_b[:], in_=b3_col[:], func=ACT.Copy, scale=0.5)
        interleave("w2")
        v_p1(0, 0, 0)
        v_p1(0, 1, 0)
        quantize("w2")
        for g in range(G):
            a_m(0, g)
        interleave("x1")
        v_p1(0, 0, 1)
        v_p1(0, 1, 1)
        products("x", 0, (2,))
        products("d", 0, (2,))
        for g in range(G):
            a_t3(0, g)
        quantize("x1")
        products("x", 1)
        v_c(0)
        v_p1(0, 0, 2)
        v_p1(0, 1, 2)
        interleave("d1", on_scalar=True)
        acts(1)
        v_b(0)
        v_w(0)
        quantize("d1")
        products("d", 1)
        v_v(0)
        v_h(0)
        v_g(0)

        def next_x(c):
            quantize("x%d" % c)
            products("x", c)
            acts(c)

        for c in range(1, CHUNKS):
            mix(c - 1)
            if c == 2:
                next_x(3)
            v_p(c, 0)
            v_p(c, 1)
            v_c(c)
            if c == 1:
                next_x(2)
            v_b(c)
            v_w(c)
            if c + 1 < CHUNKS:
                quantize("d%d" % (c + 1))
                products("d", c + 1)
            v_y(c - 1)
            v_v(c)
            v_h(c)
            if c + 1 < CHUNKS:
                v_g(c)
        c = CHUNKS - 1
        v_g(c)
        for g in range(G):
            stt(xh[c][:, g, 0, :], uu[c][:, g, 0, :], og_q[:, g : g + 1], base_sb[c][:, g, :], ALU.mult, ALU.subtract)
        for g in range(G):
            stt(yy[c][:, g, 0, :], gr[c][:, g, 0, :], og_q[:, g : g + 1], xh[c][:, g, 0, :], ALU.mult, ALU.subtract)
            nc.sync.dma_start(out=out[g, :, c * W : (c + 1) * W], in_=yy[c][:, g, 0, :])
